import numpy as np
import ml_dtypes


def mxq(x, axis, fmt="e4m3"):
    dtype, down = {"e4m3": (ml_dtypes.float8_e4m3fn, 7), "e5m2": (ml_dtypes.float8_e5m2, 14)}[fmt]
    v = np.moveaxis(np.asarray(x, np.float32).astype(ml_dtypes.bfloat16).astype(np.float64), axis, -1)
    blocks = v.reshape(v.shape[:-1] + (-1, 32))
    amax = np.abs(blocks).max(-1, keepdims=True)
    byte = np.maximum(np.where(amax > 0, np.frexp(amax)[1] - 1 + 127, 0) - down, 1)
    scale = np.exp2(byte - 127.0)
    codes = (blocks / scale).astype(np.float32).astype(dtype).astype(np.float64)
    return np.moveaxis((codes * scale).reshape(v.shape), -1, axis)


WIDE = False


def mx_kscale(k):
    if not WIDE:
        return np.ones(k)
    levels = np.array([10, -10, 5, -5, 0])
    if k % 512:
        return np.exp2(np.random.permutation(np.resize(levels, k // 32))).repeat(32)
    a = np.empty((k // 512, 16))
    for p in range(k // 512):
        a[p, :8] = np.random.permutation(np.resize(levels, 8))
        for g in range(8):
            far = levels[np.abs(levels - a[p, g]) >= 10]
            a[p, g + 8] = far[np.random.randint(len(far))]
    return np.exp2(a.ravel()).repeat(32)


def f64(x):
    return np.asarray(x).astype(np.float64)


def striped(idx):
    return np.tile(idx.reshape(-1, 16).T, (8, 1)).astype(np.uint16)


def unstriped(offs):
    return offs[:16].T.reshape(-1).astype(np.int64)


E2M1 = np.array([0.0, 0.5, 1.0, 1.5, 2.0, 3.0, 4.0, 6.0, -0.0, -0.5, -1.0, -1.5, -2.0, -3.0, -4.0, -6.0])


def pack_weight(w, fmt):
    k, n = w.shape
    w = f64(np.asarray(w, np.float32).astype(ml_dtypes.bfloat16)).reshape(k // 32, 32, n)
    amax = np.abs(w).max(1)
    if fmt == "e4m3":
        byte = np.frexp(amax)[1] - 1 + 127 - 7
    else:
        mant, ex = np.frexp(amax / 6.0)
        byte = np.where(mant > 0.5, ex, ex - 1) + 127
    byte = np.clip(np.where(amax > 0, byte, 1), 1, 254)
    scaled = (w * np.exp2(127.0 - byte)[:, None, :]).reshape(k, n).astype(np.float32)
    by_word = np.ascontiguousarray(scaled.reshape(k // 512, 128, 4, n).transpose(0, 1, 3, 2))
    if fmt == "e4m3":
        words = by_word.astype(ml_dtypes.float8_e4m3fn).view(np.uint8)
    else:
        c = by_word.astype(ml_dtypes.float4_e2m1fn).view(np.uint8) & 0xF
        words = (c[..., 0::2] | (c[..., 1::2] << 4)).reshape(k // 512, 128, 2 * n)
    return np.ascontiguousarray(words), np.ascontiguousarray(byte.astype(np.uint8).reshape(k // 512, 16, n))


def unpack_weight(words, scales, fmt):
    g, _, n = scales.shape
    words = np.ascontiguousarray(words).reshape(g, 128, n, -1)
    if fmt == "e4m3":
        vals = words.view(ml_dtypes.float8_e4m3fn).astype(np.float64)
    else:
        nib = np.empty((g, 128, n, 4), np.uint8)
        nib[..., 0::2] = words & 0xF
        nib[..., 1::2] = words >> 4
        vals = E2M1[nib]
    vals = vals * np.repeat(np.exp2(scales.astype(np.float64) - 127.0), 8, axis=1)[..., None]
    return vals.transpose(0, 1, 3, 2).reshape(g * 512, n)


def gelu(v):
    return 0.5 * v * (1.0 + np.tanh(np.sqrt(2.0 / np.pi) * (v + 0.044715 * v**3)))


def often(T, S):
    return np.random.permutation(T)[(T * np.random.uniform(0, 1, S) ** 4).astype(np.int64)]


K1, K2, T, S, H, P, N = 1024, 512, 2048, 1024, 1024, 512, 384

def setup_inputs():
    n = np.random.standard_normal
    s1, s2, s3 = mx_kscale(K1)[:, None], mx_kscale(K2)[:, None], mx_kscale(K2)[:, None]
    u = mx_kscale(H)[:, None]
    d = {}
    d["tab_words"], d["tab_scales"] = pack_weight(n((K1, T)) * s1, "e4m3")
    d["tab2_words"], d["tab2_scales"] = pack_weight(n((K2, T)) * s2, "e4m3")
    d["tab3_words"], d["tab3_scales"] = pack_weight(n((K2, T)) * s3, "e4m3")
    d["offs"] = striped(np.random.permutation(T)[:S])
    d["offs2"] = striped(np.random.permutation(T)[:S])
    d["offs3"] = striped(np.random.permutation(T)[:S])
    d["pos1"] = striped(np.random.permutation(S)[:P])
    d["pos2"] = striped(often(S, P))
    d["pos3"] = striped(often(S, P))
    d["w1"] = (n((K1, H)) / K1 ** 0.5 / s1 * u.T).astype(np.float32)
    d["w2_words"], d["w2_scales"] = pack_weight(n((K2, H)) / K2 ** 0.5 / s2 * u.T, "e2m1")
    d["w3_words"], d["w3_scales"] = pack_weight(n((K2, H)) / K2 ** 0.5 / s3 * u.T, "e4m3")
    d["allow"] = (0.8 * n((H, P)) * u).astype(np.float32)
    d["w4"] = (1.3 * n((H, N)) / H ** 0.5 / u).astype(np.float32)
    return d

def reference(tab_words, tab_scales, tab2_words, tab2_scales, tab3_words, tab3_scales, offs, offs2, offs3,
              pos1, pos2, pos3, w1, w2_words, w2_scales, w3_words, w3_scales, allow, w4):
    v = unpack_weight(tab_words, tab_scales, "e4m3")[:, unstriped(offs)]
    v2 = unpack_weight(tab2_words, tab2_scales, "e4m3")[:, unstriped(offs2)]
    v3 = unpack_weight(tab3_words, tab3_scales, "e4m3")[:, unstriped(offs3)]
    a = mxq(f64(w1), 0, "e4m3").T @ v
    b = unpack_weight(w2_words, w2_scales, "e2m1").T @ v2
    d = unpack_weight(w3_words, w3_scales, "e4m3").T @ v3
    low = np.minimum(np.minimum(a[:, unstriped(pos1)], b[:, unstriped(pos2)]), d[:, unstriped(pos3)])
    z = low + f64(allow)
    y = mxq(f64(w4), 0, "e4m3").T @ mxq(z, 0, "e4m3")
    return y / (1.0 + np.exp(-y))

@@ -1,0 +1,263 @@
+from contextlib import ExitStack
+
+import concourse.mybir as mybir
+
+K1, K2, T, S, H, PJ, N = 1024, 512, 2048, 1024, 1024, 512, 384
+FLOPS = 2 * (K1 * H * S + 2 * K2 * H * S + H * N * PJ)
+
+F32 = mybir.dt.float32
+BF16 = mybir.dt.bfloat16
+I32 = mybir.dt.int32
+U32 = mybir.dt.uint32
+U16 = mybir.dt.uint16
+U8 = mybir.dt.uint8
+FP8X4 = mybir.dt.float8_e4m3fn_x4
+FP4X4 = mybir.dt.float4_e2m1fn_x4
+MIN = mybir.AluOpType.min
+ADD = mybir.AluOpType.add
+SILU = mybir.ActivationFunctionType.Silu
+
+P = 128
+BANK = 512
+HALF = PJ // 2
+
+
+def tile_list_grain_blend_limits_kernel(
+    tc, tab_words, tab_scales, tab2_words, tab2_scales, tab3_words, tab3_scales, offs, offs2, offs3,
+    pos1, pos2, pos3, w1, w2_words, w2_scales, w3_words, w3_scales, allow, w4, out,
+):
+    nc = tc.nc
+    with ExitStack() as ctx:
+        lists = ctx.enter_context(tc.tile_pool(name="lists", bufs=1))
+        keep = ctx.enter_context(tc.tile_pool(name="keep", bufs=1))
+        big = ctx.enter_context(tc.tile_pool(name="big", bufs=4))
+        raw = ctx.enter_context(tc.tile_pool(name="raw", bufs=4))
+        cast = ctx.enter_context(tc.tile_pool(name="cast", bufs=2))
+        win_a = ctx.enter_context(tc.tile_pool(name="win_a", bufs=4))
+        win_b = ctx.enter_context(tc.tile_pool(name="win_b", bufs=5))
+        win_d = ctx.enter_context(tc.tile_pool(name="win_d", bufs=4))
+        ring = ctx.enter_context(tc.psum_pool(name="ring", bufs=5))
+        last = ctx.enter_context(tc.psum_pool(name="last", bufs=3))
+
+        def load_list(src, name):
+            t = lists.tile(list(src.shape), U16, name=name)
+            nc.sync.dma_start(t[:], src)
+            return t
+
+        def zeroed(engine, width, name):
+            t = keep.tile([P, width], U8, name=name, align_bytes=64)
+            engine.memset(t[:].bitcast(I32), 0)
+            return t
+
+        def load_scales(plane, src, first):
+            passes = src.shape[0]
+            for q in range(4):
+                rows = slice(32 * q + first, 32 * q + first + 4 * passes)
+                nc.sync.dma_start(plane[rows, :].bitcast(I32), src[:, 4 * q : 4 * q + 4, :].bitcast(I32))
+
+        def load_words(src, name):
+            t = big.tile([P, T], U32, name=name, tag="big", align_bytes=64)
+            nc.sync.dma_start(t[:].bitcast(I32), src.rearrange("p n i -> p (n i)").bitcast(I32))
+            return t
+
+        def gather(window, offsets, dtype, name):
+            t = keep.tile([P, S], dtype, name=name, align_bytes=64)
+            nc.vector.tensor_copy(t[:], window[:].indirect(offsets[:]))
+            return t
+
+        def deal(src, dtype, width, name):
+            t = keep.tile([P, width], dtype, name=name, align_bytes=64)
+            nc.vector.tensor_copy(
+                t[:].bitcast(I32).rearrange("p (b t q w) -> p b t q w", b=2, t=4, q=16),
+                src[:].bitcast(I32).rearrange("p (b q t w) -> p b t q w", b=2, t=4, q=16),
+            )
+            return t
+
+        s2_win = zeroed(nc.vector, T, "s2_win")
+        ws_raw = zeroed(nc.gpsimd, H, "ws_raw")
+        s3_win = zeroed(nc.vector, T, "s3_win")
+        s1_win = zeroed(nc.gpsimd, T, "s1_win")
+
+        o2 = load_list(offs2, "o2")
+        o3 = load_list(offs3, "o3")
+        o1 = load_list(offs, "o1")
+        p2 = load_list(pos2, "p2")
+        p3 = load_list(pos3, "p3")
+        p1 = load_list(pos1, "p1")
+        t2_win = load_words(tab2_words[0], "t2_win")
+        load_scales(s2_win, tab2_scales, 0)
+        load_scales(s3_win, tab3_scales, 0)
+        t3_win = load_words(tab3_words[0], "t3_win")
+        load_scales(ws_raw, w2_scales, 0)
+        load_scales(ws_raw, w3_scales, 4)
+        w2_raw = keep.tile([P, 2 * H], U8, name="w2_raw", align_bytes=64)
+        nc.sync.dma_start(w2_raw[:].bitcast(I32), w2_words[0].bitcast(I32))
+        w3_raw = keep.tile([P, H], U32, name="w3_raw", align_bytes=64)
+        nc.sync.dma_start(w3_raw[:].bitcast(I32), w3_words[0].rearrange("p n i -> p (n i)").bitcast(I32))
+
+        def load_w1(a, b):
+            t = raw.tile([P, 4, BANK], F32, name="w1_raw", tag="raw")
+            src = w1[512 * a : 512 * (a + 1), 512 * b : 512 * (b + 1)]
+            nc.sync.dma_start(t[:], src.rearrange("(p j) c -> p j c", j=4))
+            return t
+
+        def load_rows(t, src, b):
+            rows = src[512 * b : 512 * (b + 1), :].rearrange("(q t i) n -> t q i n", t=4, i=8)
+            for s in range(4):
+                nc.sync.dma_start(t[:, s, :], rows[s])
+
+        w1_raw = {}
+        w1_raw[0, 0] = load_w1(0, 0)
+        w1_raw[1, 0] = load_w1(1, 0)
+        load_scales(s1_win, tab_scales, 0)
+        t1_win = [load_words(tab_words[a], "t1_win%d" % a) for a in range(2)]
+        w1_raw[0, 1] = load_w1(0, 1)
+        w1_raw[1, 1] = load_w1(1, 1)
+
+        v2_w = gather(t2_win, o2, U32, "v2_w")
+        v2_s = gather(s2_win, o2, U8, "v2_s")
+        v3_s = gather(s3_win, o3, U8, "v3_s")
+        ws = deal(ws_raw, U8, H, "ws")
+        w2 = deal(w2_raw, U8, 2 * H, "w2")
+        v3_w = gather(t3_win, o3, U32, "v3_w")
+        w3 = deal(w3_raw, U32, H, "w3")
+        v1_s = gather(s1_win, o1, U8, "v1_s")
+        v1_w = [gather(t1_win[a], o1, U32, "v1_w%d" % a) for a in range(2)]
+
+        w1_bf = {}
+        w1_c = {}
+        w1_s = {}
+
+        def cast_w1(a, b):
+            t = cast.tile([P, 4 * BANK], BF16, name="w1_bf", tag="cast", align_bytes=64)
+            dst = t[:].rearrange("p (t q h i j) -> p h t q j i", t=4, q=16, h=2, i=4)
+            src = w1_raw[a, b][:].rearrange("p j (q t h i) -> p h t q j i", t=4, q=16, h=2)
+            for h in range(2):
+                nc.scalar.copy(dst[:, h], src[:, h])
+            w1_bf[a, b] = t
+
+        def quant_w1(a, b):
+            c = keep.tile([P, BANK], U32, name="w1_c%d%d" % (a, b), align_bytes=64)
+            s = keep.tile([P, BANK], U8, name="w1_s%d%d" % (a, b), align_bytes=64)
+            nc.vector.quantize_mx(out=c[:].bitcast(FP8X4), scales=s[:], in_=w1_bf[a, b][:])
+            w1_c[a, b] = c
+            w1_s[a, b] = s
+
+        def stage1(pool, name, passes):
+            window = pool.tile([P, S], F32, name=name)
+            for h in range(2):
+                cols = slice(BANK * h, BANK * (h + 1))
+                acc = ring.tile([P, BANK], F32, name="acc", tag="acc")
+                for n, (lhs, lhs_s, rhs, rhs_s, first) in enumerate(passes):
+                    nc.tensor.matmul_mx(
+                        out=acc[:], lhsT=lhs, lhsT_scale=lhs_s,
+                        rhs=rhs[:, cols].bitcast(FP8X4), rhs_scale=rhs_s[first:P, cols],
+                        start=(n == 0), stop=(n == len(passes) - 1),
+                    )
+                nc.scalar.copy(window[:, cols], acc[:])
+            return window
+
+        def make_b(s):
+            lhs = w2[:, 2 * P * s : 2 * P * (s + 1)].bitcast(FP4X4)
+            return stage1(win_b, "b", [(lhs, ws[:, P * s : P * (s + 1)], v2_w, v2_s, 0)])
+
+        def make_d(s):
+            cols = slice(P * s, P * (s + 1))
+            return stage1(win_d, "d", [(w3[:, cols].bitcast(FP8X4), ws[4:P, cols], v3_w, v3_s, 0)])
+
+        def make_a(s):
+            b, t = divmod(s, 4)
+            cols = slice(P * t, P * (t + 1))
+            return stage1(win_a, "a", [
+                (w1_c[a, b][:, cols].bitcast(FP8X4), w1_s[a, b][:, cols], v1_w[a], v1_s, 4 * a) for a in range(2)
+            ])
+
+        w4_raw = []
+        allow_sb = []
+        low = []
+        cast_w1(0, 0)
+        cast_w1(1, 0)
+        for b in range(2):
+            t = raw.tile([P, 4, N], F32, name="w4_raw", tag="raw")
+            load_rows(t, w4, b)
+            w4_raw.append(t)
+        for b in range(2):
+            t = keep.tile([P, 4, PJ], F32, name="allow%d" % b)
+            load_rows(t, allow, b)
+            allow_sb.append(t)
+
+        w4_bf = keep.tile([P, 2 * 4 * N], BF16, name="w4_bf", align_bytes=64)
+        w4_c = keep.tile([P, 2 * N], U32, name="w4_c", align_bytes=64)
+        w4_s = keep.tile([P, 2 * N], U8, name="w4_s", align_bytes=64)
+
+        def cast_w4(b):
+            dst = w4_bf[:, 4 * N * b : 4 * N * (b + 1)].rearrange("p (c i t) -> p c t i", i=4, t=4)
+            nc.scalar.copy(dst, w4_raw[b][:].rearrange("p t (c i) -> p c t i", i=4))
+
+        for b in range(2):
+            m = keep.tile([P, 4, PJ], F32, name="low%d" % b)
+            g = big.tile([P, 4, PJ], F32, name="g", tag="big", align_bytes=64)
+            for t in range(4):
+                wb = make_b(4 * b + t)
+                wd = make_d(4 * b + t)
+                nc.vector.tensor_copy(m[:, t, :], wb[:].indirect(p2[:]))
+                nc.vector.tensor_copy(g[:, t, :], wd[:].indirect(p3[:]))
+                if b == 0 and t < 2:
+                    quant_w1(t, 0)
+                if b == 0 and t >= 2:
+                    cast_w1(t - 2, 1)
+                if b == 1 and t < 2:
+                    quant_w1(t, 1)
+                if b == 1 and t >= 2:
+                    cast_w4(t - 2)
+            nc.vector.tensor_tensor(m[:], m[:], g[:], MIN)
+            low.append(m)
+
+        for c0, c1 in ((0, 512), (512, 768)):
+            nc.vector.quantize_mx(out=w4_c[:, c0:c1].bitcast(FP8X4), scales=w4_s[:, c0:c1], in_=w4_bf[:, 4 * c0 : 4 * c1])
+
+        def finish_z(b, windows, j0, j1, name):
+            width = j1 - j0
+            g = big.tile([P, 4, width], F32, name="g", tag="big", align_bytes=64)
+            for t in range(4):
+                nc.vector.tensor_copy(g[:, t, :], windows[t][:].indirect(p1[:, j0 // 16 : j1 // 16]))
+            nc.vector.tensor_tensor(g[:], g[:], low[b][:, :, j0:j1], MIN)
+            zb = cast.tile([P, 4 * width], BF16, name="zb", tag="cast", align_bytes=64)
+            nc.vector.tensor_tensor(
+                zb[:].rearrange("p (c i t) -> p c t i", i=4, t=4),
+                g[:].rearrange("p t (c i) -> p c t i", i=4),
+                allow_sb[b][:, :, j0:j1].rearrange("p t (c i) -> p c t i", i=4),
+                ADD,
+            )
+            zc = keep.tile([P, width], U32, name=name + "_c", align_bytes=64)
+            zs = keep.tile([P, width], U8, name=name + "_s", align_bytes=64)
+            nc.vector.quantize_mx(out=zc[:].bitcast(FP8X4), scales=zs[:], in_=zb[:])
+            return zc, zs
+
+        def y_pass(acc, b, n, zc, zs):
+            cols = slice(N * b + P * n, N * b + P * (n + 1))
+            nc.tensor.matmul_mx(
+                out=acc[:, 0:HALF], lhsT=w4_c[:, cols].bitcast(FP8X4), lhsT_scale=w4_s[:, cols],
+                rhs=zc.bitcast(FP8X4), rhs_scale=zs, start=(b == 0), stop=(b == 1),
+            )
+
+        def store(acc, n, j0):
+            res = keep.tile([P, HALF], F32, name="res%d_%d" % (n, j0))
+            nc.scalar.activation(res[:], acc[:, 0:HALF], SILU)
+            nc.sync.dma_start(out[P * n : P * (n + 1), j0 : j0 + HALF], res[:])
+
+        z0c, z0s = finish_z(0, [make_a(t) for t in range(4)], 0, PJ, "z0")
+        windows = [make_a(4 + t) for t in range(4)]
+        late = [last.tile([P, BANK], F32, name="late", tag="late") for n in range(3)]
+        for n in range(3):
+            y_pass(late[n], 0, n, z0c[:, HALF:PJ], z0s[:, HALF:PJ])
+        zc, zs = finish_z(1, windows, 0, HALF, "z1a")
+        for n in range(3):
+            acc = ring.tile([P, BANK], F32, name="acc", tag="acc")
+            y_pass(acc, 0, n, z0c[:, 0:HALF], z0s[:, 0:HALF])
+            y_pass(acc, 1, n, zc[:], zs[:])
+            store(acc, n, 0)
+        zc, zs = finish_z(1, windows, HALF, PJ, "z1b")
+        for n in range(3):
+            y_pass(late[n], 1, n, zc[:], zs[:])
+            store(late[n], n, HALF)

@@ -1,6 +1,7 @@
 from contextlib import ExitStack
 
 import concourse.mybir as mybir
+from concourse.masks import make_identity
 
 K1, K2, T, S, H, PJ, N = 1024, 512, 2048, 1024, 1024, 512, 384
 FLOPS = 2 * (K1 * H * S + 2 * K2 * H * S + H * N * PJ)
@@ -14,12 +15,10 @@ U8 = mybir.dt.uint8
 FP8X4 = mybir.dt.float8_e4m3fn_x4
 FP4X4 = mybir.dt.float4_e2m1fn_x4
 MIN = mybir.AluOpType.min
-ADD = mybir.AluOpType.add
 SILU = mybir.ActivationFunctionType.Silu
 
 P = 128
 BANK = 512
-HALF = PJ // 2
 
 
 def tile_list_grain_blend_limits_kernel(
@@ -30,23 +29,35 @@ def tile_list_grain_blend_limits_kernel(
     with ExitStack() as ctx:
         lists = ctx.enter_context(tc.tile_pool(name="lists", bufs=1))
         keep = ctx.enter_context(tc.tile_pool(name="keep", bufs=1))
-        big = ctx.enter_context(tc.tile_pool(name="big", bufs=4))
-        raw = ctx.enter_context(tc.tile_pool(name="raw", bufs=4))
+        big = ctx.enter_context(tc.tile_pool(name="big", bufs=1))
+        raw = ctx.enter_context(tc.tile_pool(name="raw", bufs=1))
         cast = ctx.enter_context(tc.tile_pool(name="cast", bufs=2))
+        small = ctx.enter_context(tc.tile_pool(name="small", bufs=4))
         win_a = ctx.enter_context(tc.tile_pool(name="win_a", bufs=4))
-        win_b = ctx.enter_context(tc.tile_pool(name="win_b", bufs=5))
+        win_b = ctx.enter_context(tc.tile_pool(name="win_b", bufs=4))
         win_d = ctx.enter_context(tc.tile_pool(name="win_d", bufs=4))
-        ring = ctx.enter_context(tc.psum_pool(name="ring", bufs=5))
-        last = ctx.enter_context(tc.psum_pool(name="last", bufs=3))
+        pair = ctx.enter_context(tc.tile_pool(name="pair", bufs=2))
+        psum = ctx.enter_context(tc.psum_pool(name="psum", bufs=1))
+        taken = []
+
+        def next_bank():
+            bank = psum.tile([P, BANK], F32, name="bank", tag="bank%d" % (len(taken) % 8))
+            taken.append(bank)
+            return bank
+
+        def placed(shape, dtype, name, kib):
+            return big.tile(shape, dtype, name=name, align_bytes=64, offset=1024 * kib)
 
         def load_list(src, name):
             t = lists.tile(list(src.shape), U16, name=name)
             nc.sync.dma_start(t[:], src)
             return t
 
-        def zeroed(engine, width, name):
+        def zeroed(engines, width, name):
             t = keep.tile([P, width], U8, name=name, align_bytes=64)
-            engine.memset(t[:].bitcast(I32), 0)
+            part = width // len(engines)
+            for n, engine in enumerate(engines):
+                engine.memset(t[:, part * n : part * (n + 1)].bitcast(I32), 0)
             return t
 
         def load_scales(plane, src, first):
@@ -55,99 +66,97 @@ def tile_list_grain_blend_limits_kernel(
                 rows = slice(32 * q + first, 32 * q + first + 4 * passes)
                 nc.sync.dma_start(plane[rows, :].bitcast(I32), src[:, 4 * q : 4 * q + 4, :].bitcast(I32))
 
-        def load_words(src, name):
-            t = big.tile([P, T], U32, name=name, tag="big", align_bytes=64)
+        def load_words(src, name, kib):
+            t = placed([P, T], U32, name, kib)
             nc.sync.dma_start(t[:].bitcast(I32), src.rearrange("p n i -> p (n i)").bitcast(I32))
             return t
 
-        def gather(window, offsets, dtype, name):
-            t = keep.tile([P, S], dtype, name=name, align_bytes=64)
+        def gather(window, offsets, dtype, name, kib):
+            t = placed([P, S], dtype, name, kib)
             nc.vector.tensor_copy(t[:], window[:].indirect(offsets[:]))
             return t
 
-        def deal(src, dtype, width, name):
-            t = keep.tile([P, width], dtype, name=name, align_bytes=64)
-            nc.vector.tensor_copy(
-                t[:].bitcast(I32).rearrange("p (b t q w) -> p b t q w", b=2, t=4, q=16),
-                src[:].bitcast(I32).rearrange("p (b q t w) -> p b t q w", b=2, t=4, q=16),
-            )
-            return t
-
-        s2_win = zeroed(nc.vector, T, "s2_win")
-        ws_raw = zeroed(nc.gpsimd, H, "ws_raw")
-        s3_win = zeroed(nc.vector, T, "s3_win")
-        s1_win = zeroed(nc.gpsimd, T, "s1_win")
-
-        o2 = load_list(offs2, "o2")
-        o3 = load_list(offs3, "o3")
-        o1 = load_list(offs, "o1")
-        p2 = load_list(pos2, "p2")
-        p3 = load_list(pos3, "p3")
-        p1 = load_list(pos1, "p1")
-        t2_win = load_words(tab2_words[0], "t2_win")
-        load_scales(s2_win, tab2_scales, 0)
-        load_scales(s3_win, tab3_scales, 0)
-        t3_win = load_words(tab3_words[0], "t3_win")
-        load_scales(ws_raw, w2_scales, 0)
-        load_scales(ws_raw, w3_scales, 4)
-        w2_raw = keep.tile([P, 2 * H], U8, name="w2_raw", align_bytes=64)
-        nc.sync.dma_start(w2_raw[:].bitcast(I32), w2_words[0].bitcast(I32))
-        w3_raw = keep.tile([P, H], U32, name="w3_raw", align_bytes=64)
-        nc.sync.dma_start(w3_raw[:].bitcast(I32), w3_words[0].rearrange("p n i -> p (n i)").bitcast(I32))
-
         def load_w1(a, b):
-            t = raw.tile([P, 4, BANK], F32, name="w1_raw", tag="raw")
+            t = raw.tile([P, 4, BANK], F32, name="w1_raw", tag="raw%d" % (2 * b + a), align_bytes=64)
             src = w1[512 * a : 512 * (a + 1), 512 * b : 512 * (b + 1)]
             nc.sync.dma_start(t[:], src.rearrange("(p j) c -> p j c", j=4))
             return t
 
-        def load_rows(t, src, b):
-            rows = src[512 * b : 512 * (b + 1), :].rearrange("(q t i) n -> t q i n", t=4, i=8)
-            for s in range(4):
-                nc.sync.dma_start(t[:, s, :], rows[s])
+        s2_win = zeroed([nc.vector, nc.gpsimd], T, "s2_win")
+        w2_s = zeroed([nc.gpsimd], H, "w2_s")
+        w3_s = zeroed([nc.gpsimd], H, "w3_s")
+        s3_win = zeroed([nc.vector], T, "s3_win")
+        s1_win = zeroed([nc.vector], T, "s1_win")
+        ident = keep.tile([P, P], F32, name="ident")
+        make_identity(nc, ident[:])
+        warm = keep.tile([P, 1], F32, name="warm")
+        nc.scalar.activation(warm[:], ident[:, 0:1], SILU)
 
+        o2 = load_list(offs2, "o2")
+        o3 = load_list(offs3, "o3")
+        o1 = load_list(offs, "o1")
+        load_scales(s2_win, tab2_scales, 0)
+        t2_win = load_words(tab2_words[0], "t2_win", 0)
+        load_scales(s3_win, tab3_scales, 0)
+        t3_win = load_words(tab3_words[0], "t3_win", 8)
+        w2 = keep.tile([P, 2 * H], U8, name="w2", align_bytes=64)
+        nc.sync.dma_start(w2[:].bitcast(I32), w2_words[0].bitcast(I32))
+        load_scales(w2_s, w2_scales, 0)
         w1_raw = {}
         w1_raw[0, 0] = load_w1(0, 0)
-        w1_raw[1, 0] = load_w1(1, 0)
         load_scales(s1_win, tab_scales, 0)
-        t1_win = [load_words(tab_words[a], "t1_win%d" % a) for a in range(2)]
+        t1_win = [load_words(tab_words[0], "t1_win0", 16)]
+        load_scales(w3_s, w3_scales, 0)
+        w3 = keep.tile([P, H], U32, name="w3", align_bytes=64)
+        nc.sync.dma_start(w3[:].bitcast(I32), w3_words[0].rearrange("p n i -> p (n i)").bitcast(I32))
+        t1_win.append(load_words(tab_words[1], "t1_win1", 28))
+        p2 = load_list(pos2, "p2")
+        p3 = load_list(pos3, "p3")
+        w1_raw[1, 0] = load_w1(1, 0)
         w1_raw[0, 1] = load_w1(0, 1)
         w1_raw[1, 1] = load_w1(1, 1)
+        p1 = load_list(pos1, "p1")
+        allow_sb = []
+        for b in range(2):
+            t = keep.tile([P, 4, PJ], F32, name="allow%d" % b)
+            nc.sync.dma_start(t[:], allow[512 * b : 512 * (b + 1), :].rearrange("(t p) j -> p t j", t=4))
+            allow_sb.append(t)
+        w4_raw = []
+        for b in range(2):
+            t = keep.tile([P, 4, N], F32, name="w4_raw%d" % b)
+            nc.sync.dma_start(t[:], w4[512 * b : 512 * (b + 1), :].rearrange("(p j) n -> p j n", j=4))
+            w4_raw.append(t)
 
-        v2_w = gather(t2_win, o2, U32, "v2_w")
-        v2_s = gather(s2_win, o2, U8, "v2_s")
-        v3_s = gather(s3_win, o3, U8, "v3_s")
-        ws = deal(ws_raw, U8, H, "ws")
-        w2 = deal(w2_raw, U8, 2 * H, "w2")
-        v3_w = gather(t3_win, o3, U32, "v3_w")
-        w3 = deal(w3_raw, U32, H, "w3")
-        v1_s = gather(s1_win, o1, U8, "v1_s")
-        v1_w = [gather(t1_win[a], o1, U32, "v1_w%d" % a) for a in range(2)]
+        v2_s = gather(s2_win, o2, U8, "v2_s", 44)
+        v2_w = gather(t2_win, o2, U32, "v2_w", 45)
+        v3_s = gather(s3_win, o3, U8, "v3_s", 0)
+        v3_w = gather(t3_win, o3, U32, "v3_w", 1)
+        v1_s = gather(s1_win, o1, U8, "v1_s", 8)
+        v1_w = [gather(t1_win[a], o1, U32, "v1_w%d" % a, 9 + 7 * a) for a in range(2)]
 
-        w1_bf = {}
-        w1_c = {}
-        w1_s = {}
+        def interleave(dst, src):
+            nc.scalar.copy(dst.rearrange("p (c i t) -> p c t i", i=4, t=4), src.rearrange("p t (c i) -> p c t i", i=4))
 
-        def cast_w1(a, b):
+        def quantize(src, name, c=None):
+            width = src.shape[1] // 4
+            if c is None:
+                c = keep.tile([P, width], U32, name=name + "_c", align_bytes=64)
+            s = keep.tile([P, width], U8, name=name + "_s", align_bytes=64)
+            nc.vector.quantize_mx(out=c[:].bitcast(FP8X4), scales=s[:], in_=src)
+            return c, s
+
+        w1_q = {}
+
+        def prepare_w1(a, b):
             t = cast.tile([P, 4 * BANK], BF16, name="w1_bf", tag="cast", align_bytes=64)
-            dst = t[:].rearrange("p (t q h i j) -> p h t q j i", t=4, q=16, h=2, i=4)
-            src = w1_raw[a, b][:].rearrange("p j (q t h i) -> p h t q j i", t=4, q=16, h=2)
-            for h in range(2):
-                nc.scalar.copy(dst[:, h], src[:, h])
-            w1_bf[a, b] = t
+            interleave(t[:], w1_raw[a, b][:])
+            codes = placed([P, BANK], U32, "w1_00_c", 13) if (a, b) == (0, 0) else None
+            w1_q[a, b] = quantize(t[:], "w1_%d%d" % (a, b), codes)
 
-        def quant_w1(a, b):
-            c = keep.tile([P, BANK], U32, name="w1_c%d%d" % (a, b), align_bytes=64)
-            s = keep.tile([P, BANK], U8, name="w1_s%d%d" % (a, b), align_bytes=64)
-            nc.vector.quantize_mx(out=c[:].bitcast(FP8X4), scales=s[:], in_=w1_bf[a, b][:])
-            w1_c[a, b] = c
-            w1_s[a, b] = s
-
-        def stage1(pool, name, passes):
-            window = pool.tile([P, S], F32, name=name)
+        def stage1(window, passes):
             for h in range(2):
                 cols = slice(BANK * h, BANK * (h + 1))
-                acc = ring.tile([P, BANK], F32, name="acc", tag="acc")
+                acc = next_bank()
                 for n, (lhs, lhs_s, rhs, rhs_s, first) in enumerate(passes):
                     nc.tensor.matmul_mx(
                         out=acc[:], lhsT=lhs, lhsT_scale=lhs_s,
@@ -159,105 +168,144 @@ def tile_list_grain_blend_limits_kernel(
 
         def make_b(s):
             lhs = w2[:, 2 * P * s : 2 * P * (s + 1)].bitcast(FP4X4)
-            return stage1(win_b, "b", [(lhs, ws[:, P * s : P * (s + 1)], v2_w, v2_s, 0)])
+            window = win_b.tile([P, S], F32, name="b")
+            return stage1(window, [(lhs, w2_s[:, P * s : P * (s + 1)], v2_w, v2_s, 0)])
 
         def make_d(s):
             cols = slice(P * s, P * (s + 1))
-            return stage1(win_d, "d", [(w3[:, cols].bitcast(FP8X4), ws[4:P, cols], v3_w, v3_s, 0)])
+            window = win_d.tile([P, S], F32, name="d")
+            return stage1(window, [(w3[:, cols].bitcast(FP8X4), w3_s[:, cols], v3_w, v3_s, 0)])
 
         def make_a(s):
             b, t = divmod(s, 4)
             cols = slice(P * t, P * (t + 1))
-            return stage1(win_a, "a", [
-                (w1_c[a, b][:, cols].bitcast(FP8X4), w1_s[a, b][:, cols], v1_w[a], v1_s, 4 * a) for a in range(2)
+            if b == 0:
+                window = win_a.tile([P, S], F32, name="a")
+            else:
+                window = raw.tile([P, S], F32, name="a", tag="raw%d" % t, align_bytes=64)
+            return stage1(window, [
+                (w1_q[a, b][0][:, cols].bitcast(FP8X4), w1_q[a, b][1][:, cols], v1_w[a], v1_s, 4 * a) for a in range(2)
             ])
 
-        w4_raw = []
-        allow_sb = []
-        low = []
-        cast_w1(0, 0)
-        cast_w1(1, 0)
-        for b in range(2):
-            t = raw.tile([P, 4, N], F32, name="w4_raw", tag="raw")
-            load_rows(t, w4, b)
-            w4_raw.append(t)
-        for b in range(2):
-            t = keep.tile([P, 4, PJ], F32, name="allow%d" % b)
-            load_rows(t, allow, b)
-            allow_sb.append(t)
+        def turn_plus_allow(src, b):
+            banks = [next_bank() for c in range(4)]
+            for term, first, final in ((allow_sb[b], True, False), (src, False, True)):
+                for t in range(4):
+                    for c in range(4):
+                        nc.tensor.matmul(
+                            banks[c][:, P * t : P * (t + 1)], lhsT=term[:, t, P * c : P * (c + 1)], rhs=ident[:],
+                            is_transpose=True, start=(first and t == 0), stop=(final and t == 3),
+                        )
+            return [bank[:].rearrange("j (p u e) -> j u p e", u=2, e=2) for bank in banks]
+
+        def in_pairs(ap):
+            return ap.rearrange("j (u p e) -> j u p e", u=2, e=2)
+
+        low_bd = {}
+
+        def turn_bd(b, m):
+            for c, bank in enumerate(turn_plus_allow(m, b)):
+                t = keep.tile([P, BANK], F32, name="low_bd", tag="low_bd%d%d" % (b, c), align_bytes=64)
+                nc.scalar.copy(in_pairs(t[:]), bank)
+                low_bd[b, c] = t
 
         w4_bf = keep.tile([P, 2 * 4 * N], BF16, name="w4_bf", align_bytes=64)
-        w4_c = keep.tile([P, 2 * N], U32, name="w4_c", align_bytes=64)
-        w4_s = keep.tile([P, 2 * N], U8, name="w4_s", align_bytes=64)
 
         def cast_w4(b):
-            dst = w4_bf[:, 4 * N * b : 4 * N * (b + 1)].rearrange("p (c i t) -> p c t i", i=4, t=4)
-            nc.scalar.copy(dst, w4_raw[b][:].rearrange("p t (c i) -> p c t i", i=4))
+            interleave(w4_bf[:, 4 * N * b : 4 * N * (b + 1)], w4_raw[b][:])
 
-        for b in range(2):
-            m = keep.tile([P, 4, PJ], F32, name="low%d" % b)
-            g = big.tile([P, 4, PJ], F32, name="g", tag="big", align_bytes=64)
+        wb, wd, wa = {}, {}, {}
+        m, g = {}, {}
+
+        def pick_bd(s):
+            b, t = divmod(s, 4)
+            if t == 0:
+                m[b] = placed([P, 4, PJ], F32, "m%d" % b, 28 + 8 * b)
+                g[b] = placed([P, 4, PJ], F32, "g%d" % b, 20)
+            nc.vector.tensor_copy(m[b][:, t, :], wb[s][:].indirect(p2[:]))
+            nc.vector.tensor_copy(g[b][:, t, :], wd[s][:].indirect(p3[:]))
+            if t == 3:
+                nc.vector.tensor_tensor(m[b][:], m[b][:], g[b][:], MIN)
+
+        prepare_w1(0, 0)
+        for s in range(4):
+            wb[s] = make_b(s)
+        for s in range(4):
+            wd[s] = make_d(s)
+        prepare_w1(1, 0)
+        for s in range(4):
+            pick_bd(s)
+            wb[s + 4] = make_b(s + 4)
+            wd[s + 4] = make_d(s + 4)
+            if s < 2:
+                prepare_w1(s, 1)
+            else:
+                wa[s - 2] = make_a(s - 2)
+        turn_bd(0, m[0])
+        for s in range(4, 8):
+            pick_bd(s)
+        wa[2] = make_a(2)
+        wa[3] = make_a(3)
+        for s in range(4, 8):
+            wa[s] = make_a(s)
+        turn_bd(1, m[1])
+        cast_w4(0)
+        cast_w4(1)
+
+        def w4_slice(b, n):
+            part, first = divmod(N * b + P * n, BANK)
+            c, s = w4_q[part]
+            return c[:, first : first + P].bitcast(FP8X4), s[:, first : first + P]
+
+        def pick_a(b):
+            ga = placed([P, 4, PJ], F32, "ga%d" % b, 28 - 8 * b)
             for t in range(4):
-                wb = make_b(4 * b + t)
-                wd = make_d(4 * b + t)
-                nc.vector.tensor_copy(m[:, t, :], wb[:].indirect(p2[:]))
-                nc.vector.tensor_copy(g[:, t, :], wd[:].indirect(p3[:]))
-                if b == 0 and t < 2:
-                    quant_w1(t, 0)
-                if b == 0 and t >= 2:
-                    cast_w1(t - 2, 1)
-                if b == 1 and t < 2:
-                    quant_w1(t, 1)
-                if b == 1 and t >= 2:
-                    cast_w4(t - 2)
-            nc.vector.tensor_tensor(m[:], m[:], g[:], MIN)
-            low.append(m)
+                nc.vector.tensor_copy(ga[:, t, :], wa[4 * b + t][:].indirect(p1[:]))
+            return turn_plus_allow(ga, b)
 
-        for c0, c1 in ((0, 512), (512, 768)):
-            nc.vector.quantize_mx(out=w4_c[:, c0:c1].bitcast(FP8X4), scales=w4_s[:, c0:c1], in_=w4_bf[:, 4 * c0 : 4 * c1])
+        def z_rows(b, c, bank):
+            if b == 0:
+                zt = raw.tile([P, BANK], BF16, name="zt", tag="raw%d" % c, align_bytes=64)
+            else:
+                zt = small.tile([P, BANK], BF16, name="zt", align_bytes=64)
+            nc.vector.tensor_tensor(in_pairs(zt[:]), bank, in_pairs(low_bd[b, c][:]), MIN)
+            return zt
 
-        def finish_z(b, windows, j0, j1, name):
-            width = j1 - j0
-            g = big.tile([P, 4, width], F32, name="g", tag="big", align_bytes=64)
-            for t in range(4):
-                nc.vector.tensor_copy(g[:, t, :], windows[t][:].indirect(p1[:, j0 // 16 : j1 // 16]))
-            nc.vector.tensor_tensor(g[:], g[:], low[b][:, :, j0:j1], MIN)
-            zb = cast.tile([P, 4 * width], BF16, name="zb", tag="cast", align_bytes=64)
-            nc.vector.tensor_tensor(
-                zb[:].rearrange("p (c i t) -> p c t i", i=4, t=4),
-                g[:].rearrange("p t (c i) -> p c t i", i=4),
-                allow_sb[b][:, :, j0:j1].rearrange("p t (c i) -> p c t i", i=4),
-                ADD,
-            )
-            zc = keep.tile([P, width], U32, name=name + "_c", align_bytes=64)
-            zs = keep.tile([P, width], U8, name=name + "_s", align_bytes=64)
-            nc.vector.quantize_mx(out=zc[:].bitcast(FP8X4), scales=zs[:], in_=zb[:])
-            return zc, zs
-
-        def y_pass(acc, b, n, zc, zs):
-            cols = slice(N * b + P * n, N * b + P * (n + 1))
-            nc.tensor.matmul_mx(
-                out=acc[:, 0:HALF], lhsT=w4_c[:, cols].bitcast(FP8X4), lhsT_scale=w4_s[:, cols],
-                rhs=zc.bitcast(FP8X4), rhs_scale=zs, start=(b == 0), stop=(b == 1),
+        def turn_back(zts, dst):
+            bank = next_bank()
+            for c, zt in enumerate(zts):
+                for u in range(2):
+                    at = P * (2 * c + u)
+                    nc.tensor.transpose(bank[:, at : at + P], zt[:].bitcast(F32)[:, P * u : P * (u + 1)], ident[:])
+            nc.scalar.copy(
+                dst.bitcast(F32).rearrange("p (c j u) -> p c j u", c=len(zts), u=2),
+                bank[:, 0 : 2 * P * len(zts)].rearrange("p (c u j) -> p c j u", c=len(zts), u=2),
             )
 
-        def store(acc, n, j0):
-            res = keep.tile([P, HALF], F32, name="res%d_%d" % (n, j0))
-            nc.scalar.activation(res[:], acc[:, 0:HALF], SILU)
-            nc.sync.dma_start(out[P * n : P * (n + 1), j0 : j0 + HALF], res[:])
-
-        z0c, z0s = finish_z(0, [make_a(t) for t in range(4)], 0, PJ, "z0")
-        windows = [make_a(4 + t) for t in range(4)]
-        late = [last.tile([P, BANK], F32, name="late", tag="late") for n in range(3)]
-        for n in range(3):
-            y_pass(late[n], 0, n, z0c[:, HALF:PJ], z0s[:, HALF:PJ])
-        zc, zs = finish_z(1, windows, 0, HALF, "z1a")
-        for n in range(3):
-            acc = ring.tile([P, BANK], F32, name="acc", tag="acc")
-            y_pass(acc, 0, n, z0c[:, 0:HALF], z0s[:, 0:HALF])
-            y_pass(acc, 1, n, zc[:], zs[:])
-            store(acc, n, 0)
-        zc, zs = finish_z(1, windows, HALF, PJ, "z1b")
-        for n in range(3):
-            y_pass(late[n], 1, n, zc[:], zs[:])
-            store(late[n], n, HALF)
+        banks0 = pick_a(0)
+        banks1 = pick_a(1)
+        zb0 = cast.tile([P, 4 * PJ], BF16, name="zb0", tag="cast", align_bytes=64)
+        for h in range(2):
+            zts = [z_rows(0, c, banks0[c]) for c in (2 * h, 2 * h + 1)]
+            turn_back(zts, zb0[:, 8 * P * h : 8 * P * (h + 1)])
+        w4_q = []
+        for part, (c0, c1) in enumerate(((0, 2048), (2048, 3072))):
+            codes = keep.tile([P, (c1 - c0) // 4], U32, name="w4_c", tag="low_bd0%d" % (2 + part), align_bytes=64)
+            w4_q.append(quantize(w4_bf[:, c0:c1], "w4_%d" % part, codes))
+        z0c, z0s = quantize(zb0[:], "z0")
+        for c in range(4):
+            cols = slice(P * c, P * (c + 1))
+            zb1 = pair.tile([P, 4 * P], BF16, name="zb1", align_bytes=64)
+            turn_back([z_rows(1, c, banks1[c])], zb1[:])
+            z1c, z1s = quantize(zb1[:], "z1_%d" % c)
+            acc = next_bank()
+            for n in range(3):
+                for b, (zc, zs) in enumerate(((z0c[:, cols], z0s[:, cols]), (z1c[:], z1s[:]))):
+                    lhs, lhs_s = w4_slice(b, n)
+                    nc.tensor.matmul_mx(
+                        out=acc[:, P * n : P * (n + 1)], lhsT=lhs, lhsT_scale=lhs_s,
+                        rhs=zc.bitcast(FP8X4), rhs_scale=zs, start=(b == 0), stop=(b == 1),
+                    )
+            res = small.tile([P, 3, P], F32, name="res")
+            nc.scalar.activation(res[:].rearrange("p n j -> p (n j)"), acc[:, 0:N], SILU)
+            nc.sync.dma_start(out[:, cols].rearrange("(n p) j -> p n j", p=P), res[:])

@@ -15,10 +15,21 @@ U8 = mybir.dt.uint8
 FP8X4 = mybir.dt.float8_e4m3fn_x4
 FP4X4 = mybir.dt.float4_e2m1fn_x4
 MIN = mybir.AluOpType.min
+ADD = mybir.AluOpType.add
 SILU = mybir.ActivationFunctionType.Silu
 
 P = 128
+PASS = 512
 BANK = 512
+SPLIT = PJ - P
+
+AT_TAB2, AT_TAB3, AT_TAB = 0, 8, (16, 28)
+AT_V3_SCALES, AT_V3_WORDS = 0, 1
+AT_V1_SCALES, AT_V1_WORDS = 8, (9, 16)
+AT_W1_FIRST = 13
+AT_PICKED_D = 20
+AT_LOW = (28, 36)
+AT_V2_SCALES, AT_V2_WORDS = 44, 45
 
 
 def tile_list_grain_blend_limits_kernel(
@@ -29,58 +40,53 @@ def tile_list_grain_blend_limits_kernel(
     with ExitStack() as ctx:
         lists = ctx.enter_context(tc.tile_pool(name="lists", bufs=1))
         keep = ctx.enter_context(tc.tile_pool(name="keep", bufs=1))
-        big = ctx.enter_context(tc.tile_pool(name="big", bufs=1))
+        shared = ctx.enter_context(tc.tile_pool(name="shared", bufs=1))
         raw = ctx.enter_context(tc.tile_pool(name="raw", bufs=1))
         cast = ctx.enter_context(tc.tile_pool(name="cast", bufs=2))
-        small = ctx.enter_context(tc.tile_pool(name="small", bufs=4))
+        blocks = ctx.enter_context(tc.tile_pool(name="blocks", bufs=4))
         win_a = ctx.enter_context(tc.tile_pool(name="win_a", bufs=4))
         win_b = ctx.enter_context(tc.tile_pool(name="win_b", bufs=4))
         win_d = ctx.enter_context(tc.tile_pool(name="win_d", bufs=4))
-        pair = ctx.enter_context(tc.tile_pool(name="pair", bufs=2))
         psum = ctx.enter_context(tc.psum_pool(name="psum", bufs=1))
-        taken = []
 
-        def next_bank():
-            bank = psum.tile([P, BANK], F32, name="bank", tag="bank%d" % (len(taken) % 8))
-            taken.append(bank)
-            return bank
+        def bank(n):
+            return psum.tile([P, BANK], F32, name="bank", tag="bank%d" % n)
 
         def placed(shape, dtype, name, kib):
-            return big.tile(shape, dtype, name=name, align_bytes=64, offset=1024 * kib)
+            return shared.tile(shape, dtype, name=name, align_bytes=64, offset=1024 * kib)
 
         def load_list(src, name):
-            t = lists.tile(list(src.shape), U16, name=name)
-            nc.sync.dma_start(t[:], src)
-            return t
+            tile = lists.tile(list(src.shape), U16, name=name)
+            nc.sync.dma_start(tile[:], src)
+            return tile
 
         def zeroed(engines, width, name):
-            t = keep.tile([P, width], U8, name=name, align_bytes=64)
+            tile = keep.tile([P, width], U8, name=name, align_bytes=64)
             part = width // len(engines)
             for n, engine in enumerate(engines):
-                engine.memset(t[:, part * n : part * (n + 1)].bitcast(I32), 0)
-            return t
+                engine.memset(tile[:, part * n : part * (n + 1)].bitcast(I32), 0)
+            return tile
 
-        def load_scales(plane, src, first):
+        def load_scales(tile, src):
             passes = src.shape[0]
             for q in range(4):
-                rows = slice(32 * q + first, 32 * q + first + 4 * passes)
-                nc.sync.dma_start(plane[rows, :].bitcast(I32), src[:, 4 * q : 4 * q + 4, :].bitcast(I32))
+                rows = slice(32 * q, 32 * q + 4 * passes)
+                nc.sync.dma_start(tile[rows, :].bitcast(I32), src[:, 4 * q : 4 * q + 4, :].bitcast(I32))
 
-        def load_words(src, name, kib):
-            t = placed([P, T], U32, name, kib)
-            nc.sync.dma_start(t[:].bitcast(I32), src.rearrange("p n i -> p (n i)").bitcast(I32))
-            return t
+        def load_words(tile, src):
+            nc.sync.dma_start(tile[:].bitcast(I32), src.rearrange("p n i -> p (n i)").bitcast(I32))
+            return tile
 
-        def gather(window, offsets, dtype, name, kib):
-            t = placed([P, S], dtype, name, kib)
-            nc.vector.tensor_copy(t[:], window[:].indirect(offsets[:]))
-            return t
+        def load_w1(g, half):
+            tile = raw.tile([P, 4, BANK], F32, name="w1_raw", tag="raw%d" % (2 * half + g), align_bytes=64)
+            src = w1[PASS * g : PASS * (g + 1), PASS * half : PASS * (half + 1)]
+            nc.sync.dma_start(tile[:], src.rearrange("(p j) c -> p j c", j=4))
+            return tile
 
-        def load_w1(a, b):
-            t = raw.tile([P, 4, BANK], F32, name="w1_raw", tag="raw%d" % (2 * b + a), align_bytes=64)
-            src = w1[512 * a : 512 * (a + 1), 512 * b : 512 * (b + 1)]
-            nc.sync.dma_start(t[:], src.rearrange("(p j) c -> p j c", j=4))
-            return t
+        def load_dealt_rows(tile, src):
+            rows = src[PASS : 2 * PASS, :].rearrange("(q t i) n -> t q i n", t=4, i=8)
+            for t in range(4):
+                nc.sync.dma_start(tile[:, t, :], rows[t])
 
         s2_win = zeroed([nc.vector, nc.gpsimd], T, "s2_win")
         w2_s = zeroed([nc.gpsimd], H, "w2_s")
@@ -89,223 +95,230 @@ def tile_list_grain_blend_limits_kernel(
         s1_win = zeroed([nc.vector], T, "s1_win")
         ident = keep.tile([P, P], F32, name="ident")
         make_identity(nc, ident[:])
-        warm = keep.tile([P, 1], F32, name="warm")
-        nc.scalar.activation(warm[:], ident[:, 0:1], SILU)
 
         o2 = load_list(offs2, "o2")
         o3 = load_list(offs3, "o3")
         o1 = load_list(offs, "o1")
-        load_scales(s2_win, tab2_scales, 0)
-        t2_win = load_words(tab2_words[0], "t2_win", 0)
-        load_scales(s3_win, tab3_scales, 0)
-        t3_win = load_words(tab3_words[0], "t3_win", 8)
+        load_scales(s2_win, tab2_scales)
+        t2_win = load_words(placed([P, T], U32, "t2_win", AT_TAB2), tab2_words[0])
+        load_scales(s3_win, tab3_scales)
+        t3_win = load_words(placed([P, T], U32, "t3_win", AT_TAB3), tab3_words[0])
         w2 = keep.tile([P, 2 * H], U8, name="w2", align_bytes=64)
         nc.sync.dma_start(w2[:].bitcast(I32), w2_words[0].bitcast(I32))
-        load_scales(w2_s, w2_scales, 0)
-        w1_raw = {}
-        w1_raw[0, 0] = load_w1(0, 0)
-        load_scales(s1_win, tab_scales, 0)
-        t1_win = [load_words(tab_words[0], "t1_win0", 16)]
-        load_scales(w3_s, w3_scales, 0)
-        w3 = keep.tile([P, H], U32, name="w3", align_bytes=64)
-        nc.sync.dma_start(w3[:].bitcast(I32), w3_words[0].rearrange("p n i -> p (n i)").bitcast(I32))
-        t1_win.append(load_words(tab_words[1], "t1_win1", 28))
+        load_scales(w2_s, w2_scales)
+        w1_raw = {(0, 0): load_w1(0, 0)}
+        load_scales(s1_win, tab_scales)
+        t1_win = [load_words(placed([P, T], U32, "t1_win0", AT_TAB[0]), tab_words[0])]
+        load_scales(w3_s, w3_scales)
+        w3 = load_words(keep.tile([P, H], U32, name="w3", align_bytes=64), w3_words[0])
+        t1_win.append(load_words(placed([P, T], U32, "t1_win1", AT_TAB[1]), tab_words[1]))
         p2 = load_list(pos2, "p2")
         p3 = load_list(pos3, "p3")
-        w1_raw[1, 0] = load_w1(1, 0)
-        w1_raw[0, 1] = load_w1(0, 1)
-        w1_raw[1, 1] = load_w1(1, 1)
+        for g, half in ((1, 0), (0, 1), (1, 1)):
+            w1_raw[g, half] = load_w1(g, half)
         p1 = load_list(pos1, "p1")
-        allow_sb = []
-        for b in range(2):
-            t = keep.tile([P, 4, PJ], F32, name="allow%d" % b)
-            nc.sync.dma_start(t[:], allow[512 * b : 512 * (b + 1), :].rearrange("(t p) j -> p t j", t=4))
-            allow_sb.append(t)
-        w4_raw = []
-        for b in range(2):
-            t = keep.tile([P, 4, N], F32, name="w4_raw%d" % b)
-            nc.sync.dma_start(t[:], w4[512 * b : 512 * (b + 1), :].rearrange("(p j) n -> p j n", j=4))
-            w4_raw.append(t)
+        allow_sb = [keep.tile([P, 4, PJ], F32, name="allow%d" % g) for g in range(2)]
+        w4_raw = [keep.tile([P, 4, N], F32, name="w4_raw%d" % g) for g in range(2)]
+        nc.sync.dma_start(allow_sb[0][:], allow[0:PASS, :].rearrange("(t p) j -> p t j", t=4))
+        nc.sync.dma_start(w4_raw[0][:], w4[0:PASS, :].rearrange("(p t) n -> p t n", t=4))
+        load_dealt_rows(w4_raw[1], w4)
+        load_dealt_rows(allow_sb[1], allow)
 
-        v2_s = gather(s2_win, o2, U8, "v2_s", 44)
-        v2_w = gather(t2_win, o2, U32, "v2_w", 45)
-        v3_s = gather(s3_win, o3, U8, "v3_s", 0)
-        v3_w = gather(t3_win, o3, U32, "v3_w", 1)
-        v1_s = gather(s1_win, o1, U8, "v1_s", 8)
-        v1_w = [gather(t1_win[a], o1, U32, "v1_w%d" % a, 9 + 7 * a) for a in range(2)]
+        def gather(window, offsets, dtype, name, kib):
+            tile = placed([P, S], dtype, name, kib)
+            nc.vector.tensor_copy(tile[:], window[:].indirect(offsets[:]))
+            return tile
 
-        def interleave(dst, src):
-            nc.scalar.copy(dst.rearrange("p (c i t) -> p c t i", i=4, t=4), src.rearrange("p t (c i) -> p c t i", i=4))
+        def deal(src, dtype, name):
+            width = src.shape[1] // 2
+            tile = keep.tile([P, width], dtype, name=name, align_bytes=64)
+            nc.vector.tensor_copy(
+                tile[:].bitcast(I32).rearrange("p (t q w) -> p t q w", t=4, q=16),
+                src[:, width : 2 * width].bitcast(I32).rearrange("p (q t w) -> p t q w", t=4, q=16),
+            )
+            return tile
 
-        def quantize(src, name, c=None):
+        v2_s = gather(s2_win, o2, U8, "v2_s", AT_V2_SCALES)
+        v2_w = gather(t2_win, o2, U32, "v2_w", AT_V2_WORDS)
+        v3_s = gather(s3_win, o3, U8, "v3_s", AT_V3_SCALES)
+        v3_w = gather(t3_win, o3, U32, "v3_w", AT_V3_WORDS)
+        v1_s = gather(s1_win, o1, U8, "v1_s", AT_V1_SCALES)
+        v1_w = [gather(t1_win[g], o1, U32, "v1_w%d" % g, AT_V1_WORDS[g]) for g in range(2)]
+        w2_halves = [(w2, w2_s), (deal(w2, U8, "w2_dealt"), deal(w2_s, U8, "w2_s_dealt"))]
+        w3_halves = [(w3, w3_s), (deal(w3, U32, "w3_dealt"), deal(w3_s, U8, "w3_s_dealt"))]
+
+        def four_side_by_side(ap):
+            return ap.rearrange("p (c i t) -> p c t i", i=4, t=4)
+
+        def four_rows(ap):
+            return ap.rearrange("p t (c i) -> p c t i", i=4)
+
+        def quantize(src, name, codes=None):
             width = src.shape[1] // 4
-            if c is None:
-                c = keep.tile([P, width], U32, name=name + "_c", align_bytes=64)
-            s = keep.tile([P, width], U8, name=name + "_s", align_bytes=64)
-            nc.vector.quantize_mx(out=c[:].bitcast(FP8X4), scales=s[:], in_=src)
-            return c, s
+            if codes is None:
+                codes = keep.tile([P, width], U32, name=name + "_c", align_bytes=64)
+            scales = keep.tile([P, width], U8, name=name + "_s", align_bytes=64)
+            nc.vector.quantize_mx(out=codes[:].bitcast(FP8X4), scales=scales[:], in_=src)
+            return codes, scales
 
         w1_q = {}
 
-        def prepare_w1(a, b):
-            t = cast.tile([P, 4 * BANK], BF16, name="w1_bf", tag="cast", align_bytes=64)
-            interleave(t[:], w1_raw[a, b][:])
-            codes = placed([P, BANK], U32, "w1_00_c", 13) if (a, b) == (0, 0) else None
-            w1_q[a, b] = quantize(t[:], "w1_%d%d" % (a, b), codes)
+        def prepare_w1(g, half):
+            tile = cast.tile([P, 4 * BANK], BF16, name="w1_bf", tag="cast", align_bytes=64)
+            if half == 0:
+                nc.scalar.copy(four_side_by_side(tile[:]), four_rows(w1_raw[g, half][:]))
+            else:
+                dst = tile[:].rearrange("p (t q h i j) -> p h t q j i", t=4, q=16, h=2, i=4)
+                src = w1_raw[g, half][:].rearrange("p j (q t h i) -> p h t q j i", t=4, q=16, h=2)
+                for h in range(2):
+                    nc.scalar.copy(dst[:, h], src[:, h])
+            codes = placed([P, BANK], U32, "w1_first_c", AT_W1_FIRST) if (g, half) == (0, 0) else None
+            w1_q[g, half] = quantize(tile[:], "w1_%d%d" % (g, half), codes)
 
-        def stage1(window, passes):
+        def first_product(window, first_bank, passes):
             for h in range(2):
                 cols = slice(BANK * h, BANK * (h + 1))
-                acc = next_bank()
-                for n, (lhs, lhs_s, rhs, rhs_s, first) in enumerate(passes):
+                acc = bank(first_bank + h)
+                for n, (lhs, lhs_s, rhs, rhs_s, scale_row) in enumerate(passes):
                     nc.tensor.matmul_mx(
                         out=acc[:], lhsT=lhs, lhsT_scale=lhs_s,
-                        rhs=rhs[:, cols].bitcast(FP8X4), rhs_scale=rhs_s[first:P, cols],
+                        rhs=rhs[:, cols].bitcast(FP8X4), rhs_scale=rhs_s[scale_row:P, cols],
                         start=(n == 0), stop=(n == len(passes) - 1),
                     )
                 nc.scalar.copy(window[:, cols], acc[:])
             return window
 
-        def make_b(s):
-            lhs = w2[:, 2 * P * s : 2 * P * (s + 1)].bitcast(FP4X4)
+        def make_b(s, first_bank):
+            half, t = divmod(s, 4)
+            words, scales = w2_halves[half]
+            lhs = words[:, 2 * P * t : 2 * P * (t + 1)].bitcast(FP4X4)
             window = win_b.tile([P, S], F32, name="b")
-            return stage1(window, [(lhs, w2_s[:, P * s : P * (s + 1)], v2_w, v2_s, 0)])
+            return first_product(window, first_bank, [(lhs, scales[:, P * t : P * (t + 1)], v2_w, v2_s, 0)])
 
-        def make_d(s):
-            cols = slice(P * s, P * (s + 1))
-            window = win_d.tile([P, S], F32, name="d")
-            return stage1(window, [(w3[:, cols].bitcast(FP8X4), w3_s[:, cols], v3_w, v3_s, 0)])
-
-        def make_a(s):
-            b, t = divmod(s, 4)
+        def make_d(s, first_bank):
+            half, t = divmod(s, 4)
+            words, scales = w3_halves[half]
             cols = slice(P * t, P * (t + 1))
-            if b == 0:
+            window = win_d.tile([P, S], F32, name="d")
+            return first_product(window, first_bank, [(words[:, cols].bitcast(FP8X4), scales[:, cols], v3_w, v3_s, 0)])
+
+        def make_a(s, first_bank):
+            half, t = divmod(s, 4)
+            cols = slice(P * t, P * (t + 1))
+            if half == 0:
                 window = win_a.tile([P, S], F32, name="a")
             else:
                 window = raw.tile([P, S], F32, name="a", tag="raw%d" % t, align_bytes=64)
-            return stage1(window, [
-                (w1_q[a, b][0][:, cols].bitcast(FP8X4), w1_q[a, b][1][:, cols], v1_w[a], v1_s, 4 * a) for a in range(2)
+            return first_product(window, first_bank, [
+                (w1_q[g, half][0][:, cols].bitcast(FP8X4), w1_q[g, half][1][:, cols], v1_w[g], v1_s, 4 * g)
+                for g in range(2)
             ])
 
-        def turn_plus_allow(src, b):
-            banks = [next_bank() for c in range(4)]
-            for term, first, final in ((allow_sb[b], True, False), (src, False, True)):
-                for t in range(4):
-                    for c in range(4):
-                        nc.tensor.matmul(
-                            banks[c][:, P * t : P * (t + 1)], lhsT=term[:, t, P * c : P * (c + 1)], rhs=ident[:],
-                            is_transpose=True, start=(first and t == 0), stop=(final and t == 3),
-                        )
-            return [bank[:].rearrange("j (p u e) -> j u p e", u=2, e=2) for bank in banks]
+        low = {}
+        picked_d = {}
 
-        def in_pairs(ap):
-            return ap.rearrange("j (u p e) -> j u p e", u=2, e=2)
-
-        low_bd = {}
-
-        def turn_bd(b, m):
-            for c, bank in enumerate(turn_plus_allow(m, b)):
-                t = keep.tile([P, BANK], F32, name="low_bd", tag="low_bd%d%d" % (b, c), align_bytes=64)
-                nc.scalar.copy(in_pairs(t[:]), bank)
-                low_bd[b, c] = t
-
-        w4_bf = keep.tile([P, 2 * 4 * N], BF16, name="w4_bf", align_bytes=64)
-
-        def cast_w4(b):
-            interleave(w4_bf[:, 4 * N * b : 4 * N * (b + 1)], w4_raw[b][:])
-
-        wb, wd, wa = {}, {}, {}
-        m, g = {}, {}
-
-        def pick_bd(s):
-            b, t = divmod(s, 4)
+        def pick_bd(s, window_b, window_d):
+            g, t = divmod(s, 4)
             if t == 0:
-                m[b] = placed([P, 4, PJ], F32, "m%d" % b, 28 + 8 * b)
-                g[b] = placed([P, 4, PJ], F32, "g%d" % b, 20)
-            nc.vector.tensor_copy(m[b][:, t, :], wb[s][:].indirect(p2[:]))
-            nc.vector.tensor_copy(g[b][:, t, :], wd[s][:].indirect(p3[:]))
+                low[g] = placed([P, 4, PJ], F32, "low%d" % g, AT_LOW[g])
+                picked_d[g] = placed([P, 4, PJ], F32, "picked_d%d" % g, AT_PICKED_D)
+            nc.vector.tensor_copy(low[g][:, t, :], window_b[:].indirect(p2[:]))
+            nc.vector.tensor_copy(picked_d[g][:, t, :], window_d[:].indirect(p3[:]))
             if t == 3:
-                nc.vector.tensor_tensor(m[b][:], m[b][:], g[b][:], MIN)
+                nc.vector.tensor_tensor(low[g][:], low[g][:], picked_d[g][:], MIN)
+
+        def make_and_pick_bd(s):
+            first_bank = 4 * (s % 2)
+            pick_bd(s, make_b(s, first_bank), make_d(s, first_bank + 2))
 
         prepare_w1(0, 0)
-        for s in range(4):
-            wb[s] = make_b(s)
-        for s in range(4):
-            wd[s] = make_d(s)
+        first_b = [make_b(s, 2 * s) for s in range(4)]
+        first_d = [make_d(s, 2 * s) for s in range(4)]
         prepare_w1(1, 0)
         for s in range(4):
-            pick_bd(s)
-            wb[s + 4] = make_b(s + 4)
-            wd[s + 4] = make_d(s + 4)
-            if s < 2:
-                prepare_w1(s, 1)
-            else:
-                wa[s - 2] = make_a(s - 2)
-        turn_bd(0, m[0])
-        for s in range(4, 8):
-            pick_bd(s)
-        wa[2] = make_a(2)
-        wa[3] = make_a(3)
-        for s in range(4, 8):
-            wa[s] = make_a(s)
-        turn_bd(1, m[1])
-        cast_w4(0)
-        cast_w4(1)
+            pick_bd(s, first_b[s], first_d[s])
+        make_and_pick_bd(4)
+        make_and_pick_bd(5)
+        prepare_w1(0, 1)
+        prepare_w1(1, 1)
 
-        def w4_slice(b, n):
-            part, first = divmod(N * b + P * n, BANK)
-            c, s = w4_q[part]
-            return c[:, first : first + P].bitcast(FP8X4), s[:, first : first + P]
+        picked_a = keep.tile([P, 4, PJ], F32, name="picked_a")
+        for t in range(4):
+            nc.vector.tensor_copy(picked_a[:, t, :], make_a(t, 2 * t)[:].indirect(p1[:]))
+        nc.vector.tensor_tensor(low[0][:], low[0][:], picked_a[:], MIN)
+        make_and_pick_bd(6)
+        make_and_pick_bd(7)
 
-        def pick_a(b):
-            ga = placed([P, 4, PJ], F32, "ga%d" % b, 28 - 8 * b)
-            for t in range(4):
-                nc.vector.tensor_copy(ga[:, t, :], wa[4 * b + t][:].indirect(p1[:]))
-            return turn_plus_allow(ga, b)
+        w4_bf = keep.tile([P, 2 * 4 * N], BF16, name="w4_bf", align_bytes=64)
+        for g in range(2):
+            nc.scalar.copy(four_side_by_side(w4_bf[:, 4 * N * g : 4 * N * (g + 1)]), four_rows(w4_raw[g][:]))
+        w4_q = [quantize(w4_bf[:, 0 : 4 * BANK], "w4_0"), quantize(w4_bf[:, 4 * BANK : 8 * N], "w4_1")]
+        last_a = [make_a(4, 0), make_a(5, 2)]
 
-        def z_rows(b, c, bank):
-            if b == 0:
-                zt = raw.tile([P, BANK], BF16, name="zt", tag="raw%d" % c, align_bytes=64)
-            else:
-                zt = small.tile([P, BANK], BF16, name="zt", align_bytes=64)
-            nc.vector.tensor_tensor(in_pairs(zt[:]), bank, in_pairs(low_bd[b, c][:]), MIN)
-            return zt
-
-        def turn_back(zts, dst):
-            bank = next_bank()
-            for c, zt in enumerate(zts):
-                for u in range(2):
-                    at = P * (2 * c + u)
-                    nc.tensor.transpose(bank[:, at : at + P], zt[:].bitcast(F32)[:, P * u : P * (u + 1)], ident[:])
+        turned = [bank(4 + c) for c in range(4)]
+        for term, opens in ((allow_sb[0], True), (low[0], False)):
+            for c in range(4):
+                for t in range(4):
+                    nc.tensor.matmul(
+                        turned[c][:, P * t : P * (t + 1)], lhsT=term[:, t, P * c : P * (c + 1)], rhs=ident[:],
+                        is_transpose=True, start=(opens and t == 0), stop=(not opens and t == 3),
+                    )
+        z0_rows = []
+        for c in range(4):
+            tile = blocks.tile([P, BANK], BF16, name="z0_rows", align_bytes=64)
             nc.scalar.copy(
-                dst.bitcast(F32).rearrange("p (c j u) -> p c j u", c=len(zts), u=2),
-                bank[:, 0 : 2 * P * len(zts)].rearrange("p (c u j) -> p c j u", c=len(zts), u=2),
+                tile[:].rearrange("j (u p e) -> j u p e", u=2, e=2),
+                turned[c][:].rearrange("j (p u e) -> j u p e", u=2, e=2),
+            )
+            z0_rows.append(tile)
+        last_a += [make_a(6, 0), make_a(7, 2)]
+        z0_bf = keep.tile([P, 4 * PJ], BF16, name="z0_bf", tag="late", align_bytes=64)
+        for h in range(2):
+            back = bank(5 + 2 * h)
+            for k in range(2):
+                words = z0_rows[2 * h + k][:].bitcast(F32)
+                for u in range(2):
+                    at = P * (2 * k + u)
+                    nc.tensor.transpose(back[:, at : at + P], words[:, P * u : P * (u + 1)], ident[:])
+            nc.scalar.copy(
+                z0_bf[:, 8 * P * h : 8 * P * (h + 1)].bitcast(F32).rearrange("p (k j u) -> p k j u", k=2, u=2),
+                back[:].rearrange("p (k u j) -> p k j u", k=2, u=2),
             )
 
-        banks0 = pick_a(0)
-        banks1 = pick_a(1)
-        zb0 = cast.tile([P, 4 * PJ], BF16, name="zb0", tag="cast", align_bytes=64)
-        for h in range(2):
-            zts = [z_rows(0, c, banks0[c]) for c in (2 * h, 2 * h + 1)]
-            turn_back(zts, zb0[:, 8 * P * h : 8 * P * (h + 1)])
-        w4_q = []
-        for part, (c0, c1) in enumerate(((0, 2048), (2048, 3072))):
-            codes = keep.tile([P, (c1 - c0) // 4], U32, name="w4_c", tag="low_bd0%d" % (2 + part), align_bytes=64)
-            w4_q.append(quantize(w4_bf[:, c0:c1], "w4_%d" % part, codes))
-        z0c, z0s = quantize(zb0[:], "z0")
-        for c in range(4):
-            cols = slice(P * c, P * (c + 1))
-            zb1 = pair.tile([P, 4 * P], BF16, name="zb1", align_bytes=64)
-            turn_back([z_rows(1, c, banks1[c])], zb1[:])
-            z1c, z1s = quantize(zb1[:], "z1_%d" % c)
-            acc = next_bank()
+        def round_z1(j0, j1, tag):
+            picked = keep.tile([P, 4, j1 - j0], F32, name="picked_last_a", tag=tag, align_bytes=64)
+            for t in range(4):
+                nc.vector.tensor_copy(picked[:, t, :], last_a[t][:].indirect(p1[:, j0 // 16 : j1 // 16]))
+            nc.vector.tensor_tensor(picked[:], picked[:], low[1][:, :, j0:j1], MIN)
+            tile = cast.tile([P, 4 * (j1 - j0)], BF16, name="z1_bf", tag="cast", align_bytes=64)
+            nc.vector.tensor_tensor(four_side_by_side(tile[:]), four_rows(picked[:]), four_rows(allow_sb[1][:, :, j0:j1]), ADD)
+            return tile
+
+        def y_pass(acc, g, codes, scales):
             for n in range(3):
-                for b, (zc, zs) in enumerate(((z0c[:, cols], z0s[:, cols]), (z1c[:], z1s[:]))):
-                    lhs, lhs_s = w4_slice(b, n)
-                    nc.tensor.matmul_mx(
-                        out=acc[:, P * n : P * (n + 1)], lhsT=lhs, lhsT_scale=lhs_s,
-                        rhs=zc.bitcast(FP8X4), rhs_scale=zs, start=(b == 0), stop=(b == 1),
-                    )
-            res = small.tile([P, 3, P], F32, name="res")
-            nc.scalar.activation(res[:].rearrange("p n j -> p (n j)"), acc[:, 0:N], SILU)
-            nc.sync.dma_start(out[:, cols].rearrange("(n p) j -> p n j", p=P), res[:])
+                part, first = divmod(N * g + P * n, BANK)
+                w4_codes, w4_scales = w4_q[part]
+                nc.tensor.matmul_mx(
+                    out=acc[:, P * n : P * (n + 1)],
+                    lhsT=w4_codes[:, first : first + P].bitcast(FP8X4), lhsT_scale=w4_scales[:, first : first + P],
+                    rhs=codes.bitcast(FP8X4), rhs_scale=scales, start=(g == 0 and n == 0), stop=(g == 1 and n == 2),
+                )
+
+        def finish(c, codes, scales):
+            y_pass(sums[c], 1, codes, scales)
+            res = blocks.tile([P, 3, P], F32, name="res")
+            nc.scalar.activation(res[:].rearrange("p n j -> p (n j)"), sums[c][:, 0:N], SILU)
+            nc.sync.dma_start(out[:, P * c : P * (c + 1)].rearrange("(n p) j -> p n j", p=P), res[:])
+
+        z1_early = round_z1(0, SPLIT, "early")
+        z0_codes, z0_scales = quantize(z0_bf[:], "z0")
+        sums = [bank(c) for c in range(4)]
+        for c in range(4):
+            y_pass(sums[c], 0, z0_codes[:, P * c : P * (c + 1)], z0_scales[:, P * c : P * (c + 1)])
+        codes, scales = quantize(z1_early[:, 0 : 8 * P], "z1_01")
+        for c in range(2):
+            finish(c, codes[:, P * c : P * (c + 1)], scales[:, P * c : P * (c + 1)])
+        codes, scales = quantize(z1_early[:, 8 * P : 12 * P], "z1_2")
+        finish(2, codes[:], scales[:])
+        codes, scales = quantize(round_z1(SPLIT, PJ, "late")[:], "z1_3")
+        finish(3, codes[:], scales[:])

from contextlib import ExitStack

import concourse.mybir as mybir
from concourse.masks import make_identity

K1, K2, T, S, H, PJ, N = 1024, 512, 2048, 1024, 1024, 512, 384
FLOPS = 2 * (K1 * H * S + 2 * K2 * H * S + H * N * PJ)

F32 = mybir.dt.float32
BF16 = mybir.dt.bfloat16
I32 = mybir.dt.int32
U32 = mybir.dt.uint32
U16 = mybir.dt.uint16
U8 = mybir.dt.uint8
FP8X4 = mybir.dt.float8_e4m3fn_x4
FP4X4 = mybir.dt.float4_e2m1fn_x4
MIN = mybir.AluOpType.min
ADD = mybir.AluOpType.add
SILU = mybir.ActivationFunctionType.Silu

P = 128
PASS = 512
BANK = 512
SPLIT = PJ - P

AT_TAB2, AT_TAB3, AT_TAB = 0, 8, (16, 28)
AT_V3_SCALES, AT_V3_WORDS = 0, 1
AT_V1_SCALES, AT_V1_WORDS = 8, (9, 16)
AT_W1_FIRST = 13
AT_PICKED_D = 20
AT_LOW = (28, 36)
AT_V2_SCALES, AT_V2_WORDS = 44, 45


def tile_list_grain_blend_limits_kernel(
    tc, tab_words, tab_scales, tab2_words, tab2_scales, tab3_words, tab3_scales, offs, offs2, offs3,
    pos1, pos2, pos3, w1, w2_words, w2_scales, w3_words, w3_scales, allow, w4, out,
):
    nc = tc.nc
    with ExitStack() as ctx:
        lists = ctx.enter_context(tc.tile_pool(name="lists", bufs=1))
        keep = ctx.enter_context(tc.tile_pool(name="keep", bufs=1))
        shared = ctx.enter_context(tc.tile_pool(name="shared", bufs=1))
        raw = ctx.enter_context(tc.tile_pool(name="raw", bufs=1))
        cast = ctx.enter_context(tc.tile_pool(name="cast", bufs=2))
        blocks = ctx.enter_context(tc.tile_pool(name="blocks", bufs=4))
        win_a = ctx.enter_context(tc.tile_pool(name="win_a", bufs=4))
        win_b = ctx.enter_context(tc.tile_pool(name="win_b", bufs=4))
        win_d = ctx.enter_context(tc.tile_pool(name="win_d", bufs=4))
        psum = ctx.enter_context(tc.psum_pool(name="psum", bufs=1))

        def bank(n):
            return psum.tile([P, BANK], F32, name="bank", tag="bank%d" % n)

        def placed(shape, dtype, name, kib):
            return shared.tile(shape, dtype, name=name, align_bytes=64, offset=1024 * kib)

        def load_list(src, name):
            tile = lists.tile(list(src.shape), U16, name=name)
            nc.sync.dma_start(tile[:], src)
            return tile

        def zeroed(engines, width, name):
            tile = keep.tile([P, width], U8, name=name, align_bytes=64)
            part = width // len(engines)
            for n, engine in enumerate(engines):
                engine.memset(tile[:, part * n : part * (n + 1)].bitcast(I32), 0)
            return tile

        def load_scales(tile, src):
            passes = src.shape[0]
            for q in range(4):
                rows = slice(32 * q, 32 * q + 4 * passes)
                nc.sync.dma_start(tile[rows, :].bitcast(I32), src[:, 4 * q : 4 * q + 4, :].bitcast(I32))

        def load_words(tile, src):
            nc.sync.dma_start(tile[:].bitcast(I32), src.rearrange("p n i -> p (n i)").bitcast(I32))
            return tile

        def load_w1(g, half):
            tile = raw.tile([P, 4, BANK], F32, name="w1_raw", tag="raw%d" % (2 * half + g), align_bytes=64)
            src = w1[PASS * g : PASS * (g + 1), PASS * half : PASS * (half + 1)]
            nc.sync.dma_start(tile[:], src.rearrange("(p j) c -> p j c", j=4))
            return tile

        def load_dealt_rows(tile, src):
            rows = src[PASS : 2 * PASS, :].rearrange("(q t i) n -> t q i n", t=4, i=8)
            for t in range(4):
                nc.sync.dma_start(tile[:, t, :], rows[t])

        s2_win = zeroed([nc.vector, nc.gpsimd], T, "s2_win")
        w2_s = zeroed([nc.gpsimd], H, "w2_s")
        w3_s = zeroed([nc.gpsimd], H, "w3_s")
        s3_win = zeroed([nc.vector], T, "s3_win")
        s1_win = zeroed([nc.vector], T, "s1_win")
        ident = keep.tile([P, P], F32, name="ident")
        make_identity(nc, ident[:])

        o2 = load_list(offs2, "o2")
        o3 = load_list(offs3, "o3")
        o1 = load_list(offs, "o1")
        load_scales(s2_win, tab2_scales)
        t2_win = load_words(placed([P, T], U32, "t2_win", AT_TAB2), tab2_words[0])
        load_scales(s3_win, tab3_scales)
        t3_win = load_words(placed([P, T], U32, "t3_win", AT_TAB3), tab3_words[0])
        w2 = keep.tile([P, 2 * H], U8, name="w2", align_bytes=64)
        nc.sync.dma_start(w2[:].bitcast(I32), w2_words[0].bitcast(I32))
        load_scales(w2_s, w2_scales)
        w1_raw = {(0, 0): load_w1(0, 0)}
        load_scales(s1_win, tab_scales)
        t1_win = [load_words(placed([P, T], U32, "t1_win0", AT_TAB[0]), tab_words[0])]
        load_scales(w3_s, w3_scales)
        w3 = load_words(keep.tile([P, H], U32, name="w3", align_bytes=64), w3_words[0])
        t1_win.append(load_words(placed([P, T], U32, "t1_win1", AT_TAB[1]), tab_words[1]))
        p2 = load_list(pos2, "p2")
        p3 = load_list(pos3, "p3")
        for g, half in ((1, 0), (0, 1), (1, 1)):
            w1_raw[g, half] = load_w1(g, half)
        p1 = load_list(pos1, "p1")
        allow_sb = [keep.tile([P, 4, PJ], F32, name="allow%d" % g) for g in range(2)]
        w4_raw = [keep.tile([P, 4, N], F32, name="w4_raw%d" % g) for g in range(2)]
        nc.sync.dma_start(allow_sb[0][:], allow[0:PASS, :].rearrange("(t p) j -> p t j", t=4))
        nc.sync.dma_start(w4_raw[0][:], w4[0:PASS, :].rearrange("(p t) n -> p t n", t=4))
        load_dealt_rows(w4_raw[1], w4)
        load_dealt_rows(allow_sb[1], allow)

        def gather(window, offsets, dtype, name, kib):
            tile = placed([P, S], dtype, name, kib)
            nc.vector.tensor_copy(tile[:], window[:].indirect(offsets[:]))
            return tile

        def deal(src, dtype, name):
            width = src.shape[1] // 2
            tile = keep.tile([P, width], dtype, name=name, align_bytes=64)
            nc.vector.tensor_copy(
                tile[:].bitcast(I32).rearrange("p (t q w) -> p t q w", t=4, q=16),
                src[:, width : 2 * width].bitcast(I32).rearrange("p (q t w) -> p t q w", t=4, q=16),
            )
            return tile

        v2_s = gather(s2_win, o2, U8, "v2_s", AT_V2_SCALES)
        v2_w = gather(t2_win, o2, U32, "v2_w", AT_V2_WORDS)
        v3_s = gather(s3_win, o3, U8, "v3_s", AT_V3_SCALES)
        v3_w = gather(t3_win, o3, U32, "v3_w", AT_V3_WORDS)
        v1_s = gather(s1_win, o1, U8, "v1_s", AT_V1_SCALES)
        v1_w = [gather(t1_win[g], o1, U32, "v1_w%d" % g, AT_V1_WORDS[g]) for g in range(2)]
        w2_halves = [(w2, w2_s), (deal(w2, U8, "w2_dealt"), deal(w2_s, U8, "w2_s_dealt"))]
        w3_halves = [(w3, w3_s), (deal(w3, U32, "w3_dealt"), deal(w3_s, U8, "w3_s_dealt"))]

        def four_side_by_side(ap):
            return ap.rearrange("p (c i t) -> p c t i", i=4, t=4)

        def four_rows(ap):
            return ap.rearrange("p t (c i) -> p c t i", i=4)

        def quantize(src, name, codes=None):
            width = src.shape[1] // 4
            if codes is None:
                codes = keep.tile([P, width], U32, name=name + "_c", align_bytes=64)
            scales = keep.tile([P, width], U8, name=name + "_s", align_bytes=64)
            nc.vector.quantize_mx(out=codes[:].bitcast(FP8X4), scales=scales[:], in_=src)
            return codes, scales

        w1_q = {}

        def prepare_w1(g, half):
            tile = cast.tile([P, 4 * BANK], BF16, name="w1_bf", tag="cast", align_bytes=64)
            if half == 0:
                nc.scalar.copy(four_side_by_side(tile[:]), four_rows(w1_raw[g, half][:]))
            else:
                dst = tile[:].rearrange("p (t q h i j) -> p h t q j i", t=4, q=16, h=2, i=4)
                src = w1_raw[g, half][:].rearrange("p j (q t h i) -> p h t q j i", t=4, q=16, h=2)
                for h in range(2):
                    nc.scalar.copy(dst[:, h], src[:, h])
            codes = placed([P, BANK], U32, "w1_first_c", AT_W1_FIRST) if (g, half) == (0, 0) else None
            w1_q[g, half] = quantize(tile[:], "w1_%d%d" % (g, half), codes)

        def first_product(window, first_bank, passes):
            for h in range(2):
                cols = slice(BANK * h, BANK * (h + 1))
                acc = bank(first_bank + h)
                for n, (lhs, lhs_s, rhs, rhs_s, scale_row) in enumerate(passes):
                    nc.tensor.matmul_mx(
                        out=acc[:], lhsT=lhs, lhsT_scale=lhs_s,
                        rhs=rhs[:, cols].bitcast(FP8X4), rhs_scale=rhs_s[scale_row:P, cols],
                        start=(n == 0), stop=(n == len(passes) - 1),
                    )
                nc.scalar.copy(window[:, cols], acc[:])
            return window

        def make_b(s, first_bank):
            half, t = divmod(s, 4)
            words, scales = w2_halves[half]
            lhs = words[:, 2 * P * t : 2 * P * (t + 1)].bitcast(FP4X4)
            window = win_b.tile([P, S], F32, name="b")
            return first_product(window, first_bank, [(lhs, scales[:, P * t : P * (t + 1)], v2_w, v2_s, 0)])

        def make_d(s, first_bank):
            half, t = divmod(s, 4)
            words, scales = w3_halves[half]
            cols = slice(P * t, P * (t + 1))
            window = win_d.tile([P, S], F32, name="d")
            return first_product(window, first_bank, [(words[:, cols].bitcast(FP8X4), scales[:, cols], v3_w, v3_s, 0)])

        def make_a(s, first_bank):
            half, t = divmod(s, 4)
            cols = slice(P * t, P * (t + 1))
            if half == 0:
                window = win_a.tile([P, S], F32, name="a")
            else:
                window = raw.tile([P, S], F32, name="a", tag="raw%d" % t, align_bytes=64)
            return first_product(window, first_bank, [
                (w1_q[g, half][0][:, cols].bitcast(FP8X4), w1_q[g, half][1][:, cols], v1_w[g], v1_s, 4 * g)
                for g in range(2)
            ])

        low = {}
        picked_d = {}

        def pick_bd(s, window_b, window_d):
            g, t = divmod(s, 4)
            if t == 0:
                low[g] = placed([P, 4, PJ], F32, "low%d" % g, AT_LOW[g])
                picked_d[g] = placed([P, 4, PJ], F32, "picked_d%d" % g, AT_PICKED_D)
            nc.vector.tensor_copy(low[g][:, t, :], window_b[:].indirect(p2[:]))
            nc.vector.tensor_copy(picked_d[g][:, t, :], window_d[:].indirect(p3[:]))
            if t == 3:
                nc.vector.tensor_tensor(low[g][:], low[g][:], picked_d[g][:], MIN)

        def make_and_pick_bd(s):
            first_bank = 4 * (s % 2)
            pick_bd(s, make_b(s, first_bank), make_d(s, first_bank + 2))

        prepare_w1(0, 0)
        first_b = [make_b(s, 2 * s) for s in range(4)]
        first_d = [make_d(s, 2 * s) for s in range(4)]
        prepare_w1(1, 0)
        for s in range(4):
            pick_bd(s, first_b[s], first_d[s])
        make_and_pick_bd(4)
        make_and_pick_bd(5)
        prepare_w1(0, 1)
        prepare_w1(1, 1)

        picked_a = keep.tile([P, 4, PJ], F32, name="picked_a")
        for t in range(4):
            nc.vector.tensor_copy(picked_a[:, t, :], make_a(t, 2 * t)[:].indirect(p1[:]))
        nc.vector.tensor_tensor(low[0][:], low[0][:], picked_a[:], MIN)
        make_and_pick_bd(6)
        make_and_pick_bd(7)

        w4_bf = keep.tile([P, 2 * 4 * N], BF16, name="w4_bf", align_bytes=64)
        for g in range(2):
            nc.scalar.copy(four_side_by_side(w4_bf[:, 4 * N * g : 4 * N * (g + 1)]), four_rows(w4_raw[g][:]))
        w4_q = [quantize(w4_bf[:, 0 : 4 * BANK], "w4_0"), quantize(w4_bf[:, 4 * BANK : 8 * N], "w4_1")]
        last_a = [make_a(4, 0), make_a(5, 2)]

        turned = [bank(4 + c) for c in range(4)]
        for term, opens in ((allow_sb[0], True), (low[0], False)):
            for c in range(4):
                for t in range(4):
                    nc.tensor.matmul(
                        turned[c][:, P * t : P * (t + 1)], lhsT=term[:, t, P * c : P * (c + 1)], rhs=ident[:],
                        is_transpose=True, start=(opens and t == 0), stop=(not opens and t == 3),
                    )
        z0_rows = []
        for c in range(4):
            tile = blocks.tile([P, BANK], BF16, name="z0_rows", align_bytes=64)
            nc.scalar.copy(
                tile[:].rearrange("j (u p e) -> j u p e", u=2, e=2),
                turned[c][:].rearrange("j (p u e) -> j u p e", u=2, e=2),
            )
            z0_rows.append(tile)
        last_a += [make_a(6, 0), make_a(7, 2)]
        z0_bf = keep.tile([P, 4 * PJ], BF16, name="z0_bf", tag="late", align_bytes=64)
        for h in range(2):
            back = bank(5 + 2 * h)
            for k in range(2):
                words = z0_rows[2 * h + k][:].bitcast(F32)
                for u in range(2):
                    at = P * (2 * k + u)
                    nc.tensor.transpose(back[:, at : at + P], words[:, P * u : P * (u + 1)], ident[:])
            nc.scalar.copy(
                z0_bf[:, 8 * P * h : 8 * P * (h + 1)].bitcast(F32).rearrange("p (k j u) -> p k j u", k=2, u=2),
                back[:].rearrange("p (k u j) -> p k j u", k=2, u=2),
            )

        def round_z1(j0, j1, tag):
            picked = keep.tile([P, 4, j1 - j0], F32, name="picked_last_a", tag=tag, align_bytes=64)
            for t in range(4):
                nc.vector.tensor_copy(picked[:, t, :], last_a[t][:].indirect(p1[:, j0 // 16 : j1 // 16]))
            nc.vector.tensor_tensor(picked[:], picked[:], low[1][:, :, j0:j1], MIN)
            tile = cast.tile([P, 4 * (j1 - j0)], BF16, name="z1_bf", tag="cast", align_bytes=64)
            nc.vector.tensor_tensor(four_side_by_side(tile[:]), four_rows(picked[:]), four_rows(allow_sb[1][:, :, j0:j1]), ADD)
            return tile

        def y_pass(acc, g, codes, scales):
            for n in range(3):
                part, first = divmod(N * g + P * n, BANK)
                w4_codes, w4_scales = w4_q[part]
                nc.tensor.matmul_mx(
                    out=acc[:, P * n : P * (n + 1)],
                    lhsT=w4_codes[:, first : first + P].bitcast(FP8X4), lhsT_scale=w4_scales[:, first : first + P],
                    rhs=codes.bitcast(FP8X4), rhs_scale=scales, start=(g == 0 and n == 0), stop=(g == 1 and n == 2),
                )

        def finish(c, codes, scales):
            y_pass(sums[c], 1, codes, scales)
            res = blocks.tile([P, 3, P], F32, name="res")
            nc.scalar.activation(res[:].rearrange("p n j -> p (n j)"), sums[c][:, 0:N], SILU)
            nc.sync.dma_start(out[:, P * c : P * (c + 1)].rearrange("(n p) j -> p n j", p=P), res[:])

        z1_early = round_z1(0, SPLIT, "early")
        z0_codes, z0_scales = quantize(z0_bf[:], "z0")
        sums = [bank(c) for c in range(4)]
        for c in range(4):
            y_pass(sums[c], 0, z0_codes[:, P * c : P * (c + 1)], z0_scales[:, P * c : P * (c + 1)])
        codes, scales = quantize(z1_early[:, 0 : 8 * P], "z1_01")
        for c in range(2):
            finish(c, codes[:, P * c : P * (c + 1)], scales[:, P * c : P * (c + 1)])
        codes, scales = quantize(z1_early[:, 8 * P : 12 * P], "z1_2")
        finish(2, codes[:], scales[:])
        codes, scales = quantize(round_z1(SPLIT, PJ, "late")[:], "z1_3")
        finish(3, codes[:], scales[:])
